import numpy as np
import ml_dtypes


def mxq(x, axis, fmt="e4m3"):
    dtype, down = {"e4m3": (ml_dtypes.float8_e4m3fn, 7), "e5m2": (ml_dtypes.float8_e5m2, 14)}[fmt]
    v = np.moveaxis(np.asarray(x, np.float32).astype(ml_dtypes.bfloat16).astype(np.float64), axis, -1)
    blocks = v.reshape(v.shape[:-1] + (-1, 32))
    amax = np.abs(blocks).max(-1, keepdims=True)
    byte = np.maximum(np.where(amax > 0, np.frexp(amax)[1] - 1 + 127, 0) - down, 1)
    scale = np.exp2(byte - 127.0)
    codes = (blocks / scale).astype(np.float32).astype(dtype).astype(np.float64)
    return np.moveaxis((codes * scale).reshape(v.shape), -1, axis)


WIDE = False


def mx_kscale(k):
    if not WIDE:
        return np.ones(k)
    levels = np.array([10, -10, 5, -5, 0])
    if k % 512:
        return np.exp2(np.random.permutation(np.resize(levels, k // 32))).repeat(32)
    a = np.empty((k // 512, 16))
    for p in range(k // 512):
        a[p, :8] = np.random.permutation(np.resize(levels, 8))
        for g in range(8):
            far = levels[np.abs(levels - a[p, g]) >= 10]
            a[p, g + 8] = far[np.random.randint(len(far))]
    return np.exp2(a.ravel()).repeat(32)


def f64(x):
    return np.asarray(x).astype(np.float64)


def striped8(idx):
    return np.asarray(idx).reshape(8, -1, 16).transpose(0, 2, 1).reshape(128, -1).astype(np.uint16)


def unstriped8(offs):
    return offs.reshape(8, 16, -1).transpose(0, 2, 1).reshape(8, -1).astype(np.int64)


def pick8(x, idx, run):
    r = np.arange(len(x))
    return x[r[:, None], idx[r % (8 * run) // run]]


E2M1 = np.array([0.0, 0.5, 1.0, 1.5, 2.0, 3.0, 4.0, 6.0, -0.0, -0.5, -1.0, -1.5, -2.0, -3.0, -4.0, -6.0])


def pack_weight(w, fmt):
    k, n = w.shape
    w = f64(np.asarray(w, np.float32).astype(ml_dtypes.bfloat16)).reshape(k // 32, 32, n)
    amax = np.abs(w).max(1)
    if fmt == "e4m3":
        byte = np.frexp(amax)[1] - 1 + 127 - 7
    else:
        mant, ex = np.frexp(amax / 6.0)
        byte = np.where(mant > 0.5, ex, ex - 1) + 127
    byte = np.clip(np.where(amax > 0, byte, 1), 1, 254)
    scaled = (w * np.exp2(127.0 - byte)[:, None, :]).reshape(k, n).astype(np.float32)
    by_word = np.ascontiguousarray(scaled.reshape(k // 512, 128, 4, n).transpose(0, 1, 3, 2))
    if fmt == "e4m3":
        words = by_word.astype(ml_dtypes.float8_e4m3fn).view(np.uint8)
    else:
        c = by_word.astype(ml_dtypes.float4_e2m1fn).view(np.uint8) & 0xF
        words = (c[..., 0::2] | (c[..., 1::2] << 4)).reshape(k // 512, 128, 2 * n)
    return np.ascontiguousarray(words), np.ascontiguousarray(byte.astype(np.uint8).reshape(k // 512, 16, n))


def unpack_weight(words, scales, fmt):
    g, _, n = scales.shape
    words = np.ascontiguousarray(words).reshape(g, 128, n, -1)
    if fmt == "e4m3":
        vals = words.view(ml_dtypes.float8_e4m3fn).astype(np.float64)
    else:
        nib = np.empty((g, 128, n, 4), np.uint8)
        nib[..., 0::2] = words & 0xF
        nib[..., 1::2] = words >> 4
        vals = E2M1[nib]
    vals = vals * np.repeat(np.exp2(scales.astype(np.float64) - 127.0), 8, axis=1)[..., None]
    return vals.transpose(0, 1, 3, 2).reshape(g * 512, n)


D, T, U, I, Q = 512, 1024, 1024, 512, 128


def setup_inputs():
    n = np.random.standard_normal
    idx = np.stack([np.random.permutation(T)[:I] for _ in range(8)])
    idx2 = np.stack([np.random.permutation(U)[:I] for _ in range(8)])
    idx3 = np.stack([np.random.permutation(U)[:I] for _ in range(8)])
    idx4 = np.stack([np.random.permutation(U)[:I] for _ in range(8)])
    idx5 = np.stack([np.random.permutation(T)[:I] for _ in range(8)])
    idx6 = np.stack([np.random.permutation(T)[:I] for _ in range(8)])
    fd = mx_kscale(D)
    cachep = pack_weight(n((D, T)) / fd[:, None], "e4m3")
    draftp = pack_weight(n((D, U)) / fd[:, None], "e2m1")
    return {
        "query": (n((D, Q)) * 1.0 / np.sqrt(D) * fd[:, None]).astype(np.float32),
        "cache_words": cachep[0],
        "cache_scales": cachep[1],
        "draft_words": draftp[0],
        "draft_scales": draftp[1],
        "offs": striped8(idx),
        "offs2": striped8(idx2),
        "offs3": striped8(idx3),
        "offs4": striped8(idx4),
        "offs5": striped8(idx5),
        "offs6": striped8(idx6),
    }


def reference(query, cache_words, cache_scales, draft_words, draft_scales, offs, offs2, offs3, offs4, offs5, offs6):
    idx = unstriped8(offs)
    idx2 = unstriped8(offs2)
    idx3 = unstriped8(offs3)
    idx4 = unstriped8(offs4)
    idx5 = unstriped8(offs5)
    idx6 = unstriped8(offs6)
    cacheu = unpack_weight(cache_words, cache_scales, "e4m3")
    draftu = unpack_weight(draft_words, draft_scales, "e2m1")
    queryq = mxq(f64(query), 0, "e4m3")
    a = queryq.T @ cacheu
    b = queryq.T @ draftu
    w = np.maximum(pick8(a, idx, 16), pick8(b, idx2, 16))
    w1 = np.pad(w, ((0, 0), (64, 0)))[:, :I]
    v = w - w1
    f1 = np.zeros((Q, U))
    f1[np.arange(Q)[:, None], idx3[np.arange(Q) % 128 // 16]] = w1
    bb = b + f1
    r = pick8(bb, idx4, 16) - v
    f2 = np.zeros((Q, T))
    f2[np.arange(Q)[:, None], idx5[np.arange(Q) % 128 // 16]] = r
    aa = a - f2
    y = pick8(aa, idx6, 16) + w
    return y

@@ -1,0 +1,185 @@
+from contextlib import ExitStack
+
+import concourse.mybir as mybir
+
+F32 = mybir.dt.float32
+BF16 = mybir.dt.bfloat16
+I32 = mybir.dt.int32
+U32 = mybir.dt.uint32
+U16 = mybir.dt.uint16
+U8 = mybir.dt.uint8
+FP8X4 = mybir.dt.float8_e4m3fn_x4
+FP4X4 = mybir.dt.float4_e2m1fn_x4
+COPY = mybir.ActivationFunctionType.Copy
+ADD = mybir.AluOpType.add
+SUBTRACT = mybir.AluOpType.subtract
+MAX = mybir.AluOpType.max
+
+P = 128
+PACK = 4
+D, TOKENS, SLOTS, ROWS = 512, 1024, 512, 128
+SHIFT = 64
+HALF = SLOTS // 2
+STRIPE = 16
+VECTOR_ROWS = 96
+FIRST_MAX = 96
+
+FLOPS = 2 * 2 * D * TOKENS * ROWS
+
+
+def entries(offsets, first, last):
+    return offsets[:, first // STRIPE : last // STRIPE]
+
+
+def tile_attend_pagesback_two_kernel(
+    tc, query, cache_words, cache_scales, draft_words, draft_scales, offs, offs2, offs3, offs4, offs5, offs6, out
+):
+    nc = tc.nc
+    with ExitStack() as ctx:
+        keep = ctx.enter_context(tc.tile_pool(name="keep", bufs=1))
+        psum = ctx.enter_context(tc.psum_pool(name="psum", bufs=1))
+
+        def load_scale_rows(scales, name):
+            staged = keep.tile([P, 2, TOKENS // 4], I32, name=name, tag=name)
+            for half in range(2):
+                rows = scales[0, 8 * half : 8 * half + 8, :].bitcast(I32)
+                nc.sync.dma_start(
+                    out=staged[64 * half : 64 * half + 4, :, :], in_=rows.rearrange("(q r) c -> r q c", r=4)
+                )
+            return staged
+
+        def load_list(source, name):
+            offsets = keep.tile([P, SLOTS // STRIPE], U16, name=name)
+            nc.sync.dma_start(offsets[:], source)
+            return offsets
+
+        q_raw = keep.tile([P, PACK, ROWS], F32)
+        nc.sync.dma_start(out=q_raw[:], in_=query.rearrange("(p t) q -> p t q", t=PACK))
+        draft_staged = load_scale_rows(draft_scales, "draft_staged")
+        draft_codes = keep.tile([P, 2 * TOKENS], U8, align_bytes=64)
+        nc.sync.dma_start(out=draft_codes[:].bitcast(I32), in_=draft_words[0].bitcast(I32))
+        cache_staged = load_scale_rows(cache_scales, "cache_staged")
+        cache_codes = keep.tile([P, TOKENS], I32, align_bytes=64)
+        nc.sync.dma_start(out=cache_codes[:], in_=cache_words[0].rearrange("p n t -> p (n t)").bitcast(I32))
+        list3 = load_list(offs3, "list3")
+        list2 = load_list(offs2, "list2")
+        list1 = load_list(offs, "list1")
+        list4 = load_list(offs4, "list4")
+        list5 = load_list(offs5, "list5")
+        list6 = load_list(offs6, "list6")
+
+        draft_plane = keep.tile([P, TOKENS], U8, align_bytes=64)
+        cache_plane = keep.tile([P, TOKENS], U8, align_bytes=64)
+        w_padded = keep.tile([P, SHIFT + SLOTS], F32)
+        f1_early = keep.tile([P, TOKENS], F32, tag="early_window")
+        f1_late = keep.tile([P, TOKENS], F32, tag="late_window")
+        nc.vector.memset(draft_plane[:].bitcast(I32), 0)
+        nc.vector.memset(cache_plane[:].bitcast(I32), 0)
+        nc.vector.memset(w_padded[:, 0:SHIFT], 0.0)
+        nc.vector.memset(f1_early[:], 0.0)
+        nc.vector.memset(f1_late[:], 0.0)
+        w = w_padded[:, SHIFT : SHIFT + SLOTS]
+        w1 = w_padded[:, 0:SLOTS]
+
+        q_grouped = keep.tile([P, ROWS, PACK], BF16, align_bytes=64)
+        grouped_view = q_grouped[:].rearrange("p (c i) t -> p c t i", i=4)
+        raw_view = q_raw[:].rearrange("p t (c i) -> p c t i", i=4)
+        cut = VECTOR_ROWS // 4
+        nc.scalar.activation(grouped_view[:, cut:], raw_view[:, cut:], COPY)
+        nc.vector.tensor_copy(grouped_view[:, :cut], raw_view[:, :cut])
+
+        draft_plane_words = draft_plane[:].bitcast(I32)
+        for base in (0, 64):
+            nc.vector.tensor_copy(draft_plane_words[base + 32 : base + 36, :], draft_staged[base : base + 4, 1, :])
+            nc.scalar.copy(
+                draft_plane[base : base + 4, :].bitcast(U32), draft_staged[base : base + 4, 0, :].bitcast(U32)
+            )
+
+        q_codes = keep.tile([P, ROWS], U32, align_bytes=64)
+        q_plane = keep.tile([P, ROWS], U8, align_bytes=64)
+        nc.vector.quantize_mx(
+            out=q_codes[:].bitcast(FP8X4), scales=q_plane[:], in_=q_grouped[:].rearrange("p q t -> p (q t)")
+        )
+
+        nc.scalar.activation(f1_late[:].indirect(entries(list3, 0, SHIFT)), w1[:, 0:SHIFT], COPY)
+
+        cache_plane_words = cache_plane[:].bitcast(I32)
+        for base in (0, 64):
+            for quarter in range(2):
+                first = base + 32 * quarter
+                nc.vector.tensor_copy(cache_plane_words[first : first + 4, :], cache_staged[base : base + 4, quarter, :])
+
+        def score(first, last, codes, plane, name):
+            bank = psum.tile([P, last - first], F32, name=name)
+            nc.tensor.matmul_mx(
+                out=bank[:],
+                lhsT=q_codes[:].bitcast(FP8X4),
+                lhsT_scale=q_plane[:],
+                rhs=codes,
+                rhs_scale=plane[:, first:last],
+                start=True,
+                stop=True,
+            )
+            return bank
+
+        b = keep.tile([P, TOKENS], F32, tag="cache_staged")
+        for first, last in ((0, 512), (512, 768), (768, 1024)):
+            bank = score(first, last, draft_codes[:, 2 * first : 2 * last].bitcast(FP4X4), draft_plane, f"b{first}")
+            if first == 0:
+                nc.vector.tensor_copy(b[:, first:last], bank[:])
+            else:
+                nc.scalar.copy(b[:, first:last], bank[:])
+
+        b_listed = keep.tile([P, SLOTS], F32)
+        nc.vector.tensor_copy(b_listed[:], b[:].indirect(list2[:]))
+
+        a = keep.tile([P, TOKENS], F32)
+        for first in range(0, TOKENS, 256):
+            last = first + 256
+            bank = score(first, last, cache_codes[:, first:last].bitcast(FP8X4), cache_plane, f"a{first}")
+            nc.scalar.copy(a[:, first:last], bank[:])
+
+        a_low = keep.tile([P, HALF], F32)
+        a_high = keep.tile([P, HALF], F32)
+        nc.vector.tensor_copy(a_low[:], a[:].indirect(entries(list1, 0, HALF)))
+        nc.scalar.activation(a_high[:], a[:].indirect(entries(list1, HALF, SLOTS)), COPY)
+
+        nc.vector.tensor_tensor(w[:, 0:FIRST_MAX], a_low[:, 0:FIRST_MAX], b_listed[:, 0:FIRST_MAX], MAX)
+        split = SHIFT + FIRST_MAX
+        nc.scalar.activation(f1_early[:].indirect(entries(list3, SHIFT, split)), w1[:, SHIFT:split], COPY)
+        nc.vector.tensor_tensor(w[:, FIRST_MAX:HALF], a_low[:, FIRST_MAX:HALF], b_listed[:, FIRST_MAX:HALF], MAX)
+        nc.vector.tensor_tensor(w[:, HALF:SLOTS], a_high[:], b_listed[:, HALF:SLOTS], MAX)
+        nc.scalar.activation(f1_late[:].indirect(entries(list3, split, SLOTS)), w1[:, split:SLOTS], COPY)
+
+        v = keep.tile([P, SLOTS], F32)
+        nc.vector.tensor_tensor(v[:], w, w1, SUBTRACT)
+
+        b_early = keep.tile([P, TOKENS], F32)
+        nc.vector.tensor_tensor(b_early[:], b[:], f1_early[:], ADD)
+        f2_early = keep.tile([P, TOKENS], F32, tag="early_window")
+        nc.gpsimd.memset(f2_early[:], 0.0)
+        bb = keep.tile([P, TOKENS], F32)
+        nc.vector.tensor_tensor(bb[:], b_early[:], f1_late[:], ADD)
+
+        r_low = keep.tile([P, HALF], F32)
+        r_high = keep.tile([P, HALF], F32)
+        nc.vector.tensor_tensor(r_low[:], bb[:].indirect(entries(list4, 0, HALF)), v[:, 0:HALF], SUBTRACT)
+        nc.scalar.activation(f2_early[:].indirect(entries(list5, 0, HALF)), r_low[:], COPY)
+        nc.vector.tensor_tensor(r_high[:], bb[:].indirect(entries(list4, HALF, SLOTS)), v[:, HALF:SLOTS], SUBTRACT)
+        f2_late = keep.tile([P, TOKENS], F32, tag="late_window")
+        nc.gpsimd.memset(f2_late[:], 0.0)
+        nc.scalar.activation(f2_late[:].indirect(entries(list5, HALF, SLOTS)), r_high[:], COPY)
+
+        a_early = keep.tile([P, TOKENS], F32)
+        nc.vector.tensor_tensor(a_early[:], a[:], f2_early[:], SUBTRACT)
+        aa = keep.tile([P, TOKENS], F32)
+        nc.vector.tensor_tensor(aa[:], a_early[:], f2_late[:], SUBTRACT)
+
+        y_low = keep.tile([P, HALF], F32)
+        aa_high = keep.tile([P, HALF], F32)
+        y_high = keep.tile([P, HALF], F32)
+        nc.vector.tensor_tensor(y_low[:], aa[:].indirect(entries(list6, 0, HALF)), w[:, 0:HALF], ADD)
+        nc.scalar.activation(aa_high[:], aa[:].indirect(entries(list6, HALF, SLOTS)), COPY)
+        nc.sync.dma_start(out=out[:, 0:HALF], in_=y_low[:])
+        nc.vector.tensor_tensor(y_high[:], aa_high[:], w[:, HALF:SLOTS], ADD)
+        nc.sync.dma_start(out=out[:, HALF:SLOTS], in_=y_high[:])

@@ -39,45 +39,42 @@ def tile_attend_pagesback_two_kernel(
         keep = ctx.enter_context(tc.tile_pool(name="keep", bufs=1))
         psum = ctx.enter_context(tc.psum_pool(name="psum", bufs=1))
 
-        def load_scale_rows(scales, name):
-            staged = keep.tile([P, 2, TOKENS // 4], I32, name=name, tag=name)
-            for half in range(2):
-                rows = scales[0, 8 * half : 8 * half + 8, :].bitcast(I32)
-                nc.sync.dma_start(
-                    out=staged[64 * half : 64 * half + 4, :, :], in_=rows.rearrange("(q r) c -> r q c", r=4)
-                )
-            return staged
+        def load_scale_plane(scales, plane):
+            rows = scales[0].bitcast(I32)
+            for r in range(4):
+                nc.sync.dma_start(out=plane[r:P:32, :].bitcast(I32), in_=rows[r:16:4, :])
 
         def load_list(source, name):
             offsets = keep.tile([P, SLOTS // STRIPE], U16, name=name)
             nc.sync.dma_start(offsets[:], source)
             return offsets
 
+        draft_plane = keep.tile([P, TOKENS], U8, align_bytes=64)
+        cache_plane = keep.tile([P, TOKENS], U8, align_bytes=64)
+        nc.vector.memset(draft_plane[:].bitcast(I32), 0)
+        nc.vector.memset(cache_plane[:].bitcast(I32), 0)
+
         q_raw = keep.tile([P, PACK, ROWS], F32)
         nc.sync.dma_start(out=q_raw[:], in_=query.rearrange("(p t) q -> p t q", t=PACK))
-        draft_staged = load_scale_rows(draft_scales, "draft_staged")
+        list3 = load_list(offs3, "list3")
+        load_scale_plane(draft_scales, draft_plane)
         draft_codes = keep.tile([P, 2 * TOKENS], U8, align_bytes=64)
         nc.sync.dma_start(out=draft_codes[:].bitcast(I32), in_=draft_words[0].bitcast(I32))
-        cache_staged = load_scale_rows(cache_scales, "cache_staged")
         cache_codes = keep.tile([P, TOKENS], I32, align_bytes=64)
         nc.sync.dma_start(out=cache_codes[:], in_=cache_words[0].rearrange("p n t -> p (n t)").bitcast(I32))
-        list3 = load_list(offs3, "list3")
+        load_scale_plane(cache_scales, cache_plane)
         list2 = load_list(offs2, "list2")
         list1 = load_list(offs, "list1")
         list4 = load_list(offs4, "list4")
         list5 = load_list(offs5, "list5")
         list6 = load_list(offs6, "list6")
 
-        draft_plane = keep.tile([P, TOKENS], U8, align_bytes=64)
-        cache_plane = keep.tile([P, TOKENS], U8, align_bytes=64)
         w_padded = keep.tile([P, SHIFT + SLOTS], F32)
         f1_early = keep.tile([P, TOKENS], F32, tag="early_window")
         f1_late = keep.tile([P, TOKENS], F32, tag="late_window")
-        nc.vector.memset(draft_plane[:].bitcast(I32), 0)
-        nc.vector.memset(cache_plane[:].bitcast(I32), 0)
         nc.vector.memset(w_padded[:, 0:SHIFT], 0.0)
-        nc.vector.memset(f1_early[:], 0.0)
         nc.vector.memset(f1_late[:], 0.0)
+        nc.vector.memset(f1_early[:], 0.0)
         w = w_padded[:, SHIFT : SHIFT + SLOTS]
         w1 = w_padded[:, 0:SLOTS]
 
@@ -88,13 +85,6 @@ def tile_attend_pagesback_two_kernel(
         nc.scalar.activation(grouped_view[:, cut:], raw_view[:, cut:], COPY)
         nc.vector.tensor_copy(grouped_view[:, :cut], raw_view[:, :cut])
 
-        draft_plane_words = draft_plane[:].bitcast(I32)
-        for base in (0, 64):
-            nc.vector.tensor_copy(draft_plane_words[base + 32 : base + 36, :], draft_staged[base : base + 4, 1, :])
-            nc.scalar.copy(
-                draft_plane[base : base + 4, :].bitcast(U32), draft_staged[base : base + 4, 0, :].bitcast(U32)
-            )
-
         q_codes = keep.tile([P, ROWS], U32, align_bytes=64)
         q_plane = keep.tile([P, ROWS], U8, align_bytes=64)
         nc.vector.quantize_mx(
@@ -102,12 +92,6 @@ def tile_attend_pagesback_two_kernel(
         )
 
         nc.scalar.activation(f1_late[:].indirect(entries(list3, 0, SHIFT)), w1[:, 0:SHIFT], COPY)
-
-        cache_plane_words = cache_plane[:].bitcast(I32)
-        for base in (0, 64):
-            for quarter in range(2):
-                first = base + 32 * quarter
-                nc.vector.tensor_copy(cache_plane_words[first : first + 4, :], cache_staged[base : base + 4, quarter, :])
 
         def score(first, last, codes, plane, name):
             bank = psum.tile([P, last - first], F32, name=name)
@@ -122,13 +106,13 @@ def tile_attend_pagesback_two_kernel(
             )
             return bank
 
-        b = keep.tile([P, TOKENS], F32, tag="cache_staged")
+        b = keep.tile([P, TOKENS], F32)
         for first, last in ((0, 512), (512, 768), (768, 1024)):
             bank = score(first, last, draft_codes[:, 2 * first : 2 * last].bitcast(FP4X4), draft_plane, f"b{first}")
             if first == 0:
-                nc.vector.tensor_copy(b[:, first:last], bank[:])
-            else:
                 nc.scalar.copy(b[:, first:last], bank[:])
+            else:
+                nc.vector.tensor_copy(b[:, first:last], bank[:])
 
         b_listed = keep.tile([P, SLOTS], F32)
         nc.vector.tensor_copy(b_listed[:], b[:].indirect(list2[:]))

@@ -61,9 +61,12 @@ def tile_attend_pagesback_two_kernel(
         draft_codes = keep.tile([P, 2 * TOKENS], U8, align_bytes=64)
         nc.sync.dma_start(out=draft_codes[:].bitcast(I32), in_=draft_words[0].bitcast(I32))
         cache_codes = keep.tile([P, TOKENS], I32, align_bytes=64)
-        nc.sync.dma_start(out=cache_codes[:], in_=cache_words[0].rearrange("p n t -> p (n t)").bitcast(I32))
+        cache_as_words = cache_words[0].rearrange("p n t -> p (n t)").bitcast(I32)
+        nc.sync.dma_start(out=cache_codes[:, 0:512], in_=cache_as_words[:, 0:512])
         load_scale_plane(cache_scales, cache_plane)
+        nc.sync.dma_start(out=cache_codes[:, 512:768], in_=cache_as_words[:, 512:768])
         list2 = load_list(offs2, "list2")
+        nc.sync.dma_start(out=cache_codes[:, 768:1024], in_=cache_as_words[:, 768:1024])
         list1 = load_list(offs, "list1")
         list4 = load_list(offs4, "list4")
         list5 = load_list(offs5, "list5")
@@ -114,14 +117,14 @@ def tile_attend_pagesback_two_kernel(
             else:
                 nc.vector.tensor_copy(b[:, first:last], bank[:])
 
-        b_listed = keep.tile([P, SLOTS], F32)
-        nc.vector.tensor_copy(b_listed[:], b[:].indirect(list2[:]))
-
         a = keep.tile([P, TOKENS], F32)
         for first in range(0, TOKENS, 256):
             last = first + 256
             bank = score(first, last, cache_codes[:, first:last].bitcast(FP8X4), cache_plane, f"a{first}")
             nc.scalar.copy(a[:, first:last], bank[:])
+
+        b_listed = keep.tile([P, SLOTS], F32)
+        nc.vector.tensor_copy(b_listed[:], b[:].indirect(list2[:]))
 
         a_low = keep.tile([P, HALF], F32)
         a_high = keep.tile([P, HALF], F32)

@@ -74,14 +74,14 @@ def tile_attend_pagesback_two_kernel(
 
         w_padded = keep.tile([P, SHIFT + SLOTS], F32)
         f1_early = keep.tile([P, TOKENS], F32, tag="early_window")
-        f1_late = keep.tile([P, TOKENS], F32, tag="late_window")
+        f1_late = keep.tile([P, TOKENS], F32)
         nc.vector.memset(w_padded[:, 0:SHIFT], 0.0)
         nc.vector.memset(f1_late[:], 0.0)
         nc.vector.memset(f1_early[:], 0.0)
         w = w_padded[:, SHIFT : SHIFT + SLOTS]
         w1 = w_padded[:, 0:SLOTS]
 
-        q_grouped = keep.tile([P, ROWS, PACK], BF16, align_bytes=64)
+        q_grouped = keep.tile([P, ROWS, PACK], BF16, align_bytes=64, tag="grouped_then_f2")
         grouped_view = q_grouped[:].rearrange("p (c i) t -> p c t i", i=4)
         raw_view = q_raw[:].rearrange("p t (c i) -> p c t i", i=4)
         cut = VECTOR_ROWS // 4
@@ -95,6 +95,9 @@ def tile_attend_pagesback_two_kernel(
         )
 
         nc.scalar.activation(f1_late[:].indirect(entries(list3, 0, SHIFT)), w1[:, 0:SHIFT], COPY)
+
+        f2_early = keep.tile([P, TOKENS], F32, align_bytes=64, tag="grouped_then_f2")
+        nc.vector.memset(f2_early[:], 0.0)
 
         def score(first, last, codes, plane, name):
             bank = psum.tile([P, last - first], F32, name=name)
@@ -143,8 +146,8 @@ def tile_attend_pagesback_two_kernel(
 
         b_early = keep.tile([P, TOKENS], F32)
         nc.vector.tensor_tensor(b_early[:], b[:], f1_early[:], ADD)
-        f2_early = keep.tile([P, TOKENS], F32, tag="early_window")
-        nc.gpsimd.memset(f2_early[:], 0.0)
+        f2_late = keep.tile([P, TOKENS], F32, tag="early_window")
+        nc.vector.memset(f2_late[:], 0.0)
         bb = keep.tile([P, TOKENS], F32)
         nc.vector.tensor_tensor(bb[:], b_early[:], f1_late[:], ADD)
 
@@ -153,8 +156,6 @@ def tile_attend_pagesback_two_kernel(
         nc.vector.tensor_tensor(r_low[:], bb[:].indirect(entries(list4, 0, HALF)), v[:, 0:HALF], SUBTRACT)
         nc.scalar.activation(f2_early[:].indirect(entries(list5, 0, HALF)), r_low[:], COPY)
         nc.vector.tensor_tensor(r_high[:], bb[:].indirect(entries(list4, HALF, SLOTS)), v[:, HALF:SLOTS], SUBTRACT)
-        f2_late = keep.tile([P, TOKENS], F32, tag="late_window")
-        nc.gpsimd.memset(f2_late[:], 0.0)
         nc.scalar.activation(f2_late[:].indirect(entries(list5, HALF, SLOTS)), r_high[:], COPY)
 
         a_early = keep.tile([P, TOKENS], F32)

from contextlib import ExitStack

import concourse.mybir as mybir

F32 = mybir.dt.float32
BF16 = mybir.dt.bfloat16
I32 = mybir.dt.int32
U32 = mybir.dt.uint32
U16 = mybir.dt.uint16
U8 = mybir.dt.uint8
FP8X4 = mybir.dt.float8_e4m3fn_x4
FP4X4 = mybir.dt.float4_e2m1fn_x4
COPY = mybir.ActivationFunctionType.Copy
ADD = mybir.AluOpType.add
SUBTRACT = mybir.AluOpType.subtract
MAX = mybir.AluOpType.max

P = 128
PACK = 4
D, TOKENS, SLOTS, ROWS = 512, 1024, 512, 128
SHIFT = 64
HALF = SLOTS // 2
STRIPE = 16
VECTOR_ROWS = 96
FIRST_MAX = 96

FLOPS = 2 * 2 * D * TOKENS * ROWS


def entries(offsets, first, last):
    return offsets[:, first // STRIPE : last // STRIPE]


def tile_attend_pagesback_two_kernel(
    tc, query, cache_words, cache_scales, draft_words, draft_scales, offs, offs2, offs3, offs4, offs5, offs6, out
):
    nc = tc.nc
    with ExitStack() as ctx:
        keep = ctx.enter_context(tc.tile_pool(name="keep", bufs=1))
        psum = ctx.enter_context(tc.psum_pool(name="psum", bufs=1))

        def load_scale_plane(scales, plane):
            rows = scales[0].bitcast(I32)
            for r in range(4):
                nc.sync.dma_start(out=plane[r:P:32, :].bitcast(I32), in_=rows[r:16:4, :])

        def load_list(source, name):
            offsets = keep.tile([P, SLOTS // STRIPE], U16, name=name)
            nc.sync.dma_start(offsets[:], source)
            return offsets

        draft_plane = keep.tile([P, TOKENS], U8, align_bytes=64)
        cache_plane = keep.tile([P, TOKENS], U8, align_bytes=64)
        nc.vector.memset(draft_plane[:].bitcast(I32), 0)
        nc.vector.memset(cache_plane[:].bitcast(I32), 0)

        q_raw = keep.tile([P, PACK, ROWS], F32)
        nc.sync.dma_start(out=q_raw[:], in_=query.rearrange("(p t) q -> p t q", t=PACK))
        list3 = load_list(offs3, "list3")
        load_scale_plane(draft_scales, draft_plane)
        draft_codes = keep.tile([P, 2 * TOKENS], U8, align_bytes=64)
        nc.sync.dma_start(out=draft_codes[:].bitcast(I32), in_=draft_words[0].bitcast(I32))
        cache_codes = keep.tile([P, TOKENS], I32, align_bytes=64)
        cache_as_words = cache_words[0].rearrange("p n t -> p (n t)").bitcast(I32)
        nc.sync.dma_start(out=cache_codes[:, 0:512], in_=cache_as_words[:, 0:512])
        load_scale_plane(cache_scales, cache_plane)
        nc.sync.dma_start(out=cache_codes[:, 512:768], in_=cache_as_words[:, 512:768])
        list2 = load_list(offs2, "list2")
        nc.sync.dma_start(out=cache_codes[:, 768:1024], in_=cache_as_words[:, 768:1024])
        list1 = load_list(offs, "list1")
        list4 = load_list(offs4, "list4")
        list5 = load_list(offs5, "list5")
        list6 = load_list(offs6, "list6")

        w_padded = keep.tile([P, SHIFT + SLOTS], F32)
        f1_early = keep.tile([P, TOKENS], F32, tag="early_window")
        f1_late = keep.tile([P, TOKENS], F32)
        nc.vector.memset(w_padded[:, 0:SHIFT], 0.0)
        nc.vector.memset(f1_late[:], 0.0)
        nc.vector.memset(f1_early[:], 0.0)
        w = w_padded[:, SHIFT : SHIFT + SLOTS]
        w1 = w_padded[:, 0:SLOTS]

        q_grouped = keep.tile([P, ROWS, PACK], BF16, align_bytes=64, tag="grouped_then_f2")
        grouped_view = q_grouped[:].rearrange("p (c i) t -> p c t i", i=4)
        raw_view = q_raw[:].rearrange("p t (c i) -> p c t i", i=4)
        cut = VECTOR_ROWS // 4
        nc.scalar.activation(grouped_view[:, cut:], raw_view[:, cut:], COPY)
        nc.vector.tensor_copy(grouped_view[:, :cut], raw_view[:, :cut])

        q_codes = keep.tile([P, ROWS], U32, align_bytes=64)
        q_plane = keep.tile([P, ROWS], U8, align_bytes=64)
        nc.vector.quantize_mx(
            out=q_codes[:].bitcast(FP8X4), scales=q_plane[:], in_=q_grouped[:].rearrange("p q t -> p (q t)")
        )

        nc.scalar.activation(f1_late[:].indirect(entries(list3, 0, SHIFT)), w1[:, 0:SHIFT], COPY)

        f2_early = keep.tile([P, TOKENS], F32, align_bytes=64, tag="grouped_then_f2")
        nc.vector.memset(f2_early[:], 0.0)

        def score(first, last, codes, plane, name):
            bank = psum.tile([P, last - first], F32, name=name)
            nc.tensor.matmul_mx(
                out=bank[:],
                lhsT=q_codes[:].bitcast(FP8X4),
                lhsT_scale=q_plane[:],
                rhs=codes,
                rhs_scale=plane[:, first:last],
                start=True,
                stop=True,
            )
            return bank

        b = keep.tile([P, TOKENS], F32)
        for first, last in ((0, 512), (512, 768), (768, 1024)):
            bank = score(first, last, draft_codes[:, 2 * first : 2 * last].bitcast(FP4X4), draft_plane, f"b{first}")
            if first == 0:
                nc.scalar.copy(b[:, first:last], bank[:])
            else:
                nc.vector.tensor_copy(b[:, first:last], bank[:])

        a = keep.tile([P, TOKENS], F32)
        for first in range(0, TOKENS, 256):
            last = first + 256
            bank = score(first, last, cache_codes[:, first:last].bitcast(FP8X4), cache_plane, f"a{first}")
            nc.scalar.copy(a[:, first:last], bank[:])

        b_listed = keep.tile([P, SLOTS], F32)
        nc.vector.tensor_copy(b_listed[:], b[:].indirect(list2[:]))

        a_low = keep.tile([P, HALF], F32)
        a_high = keep.tile([P, HALF], F32)
        nc.vector.tensor_copy(a_low[:], a[:].indirect(entries(list1, 0, HALF)))
        nc.scalar.activation(a_high[:], a[:].indirect(entries(list1, HALF, SLOTS)), COPY)

        nc.vector.tensor_tensor(w[:, 0:FIRST_MAX], a_low[:, 0:FIRST_MAX], b_listed[:, 0:FIRST_MAX], MAX)
        split = SHIFT + FIRST_MAX
        nc.scalar.activation(f1_early[:].indirect(entries(list3, SHIFT, split)), w1[:, SHIFT:split], COPY)
        nc.vector.tensor_tensor(w[:, FIRST_MAX:HALF], a_low[:, FIRST_MAX:HALF], b_listed[:, FIRST_MAX:HALF], MAX)
        nc.vector.tensor_tensor(w[:, HALF:SLOTS], a_high[:], b_listed[:, HALF:SLOTS], MAX)
        nc.scalar.activation(f1_late[:].indirect(entries(list3, split, SLOTS)), w1[:, split:SLOTS], COPY)

        v = keep.tile([P, SLOTS], F32)
        nc.vector.tensor_tensor(v[:], w, w1, SUBTRACT)

        b_early = keep.tile([P, TOKENS], F32)
        nc.vector.tensor_tensor(b_early[:], b[:], f1_early[:], ADD)
        f2_late = keep.tile([P, TOKENS], F32, tag="early_window")
        nc.vector.memset(f2_late[:], 0.0)
        bb = keep.tile([P, TOKENS], F32)
        nc.vector.tensor_tensor(bb[:], b_early[:], f1_late[:], ADD)

        r_low = keep.tile([P, HALF], F32)
        r_high = keep.tile([P, HALF], F32)
        nc.vector.tensor_tensor(r_low[:], bb[:].indirect(entries(list4, 0, HALF)), v[:, 0:HALF], SUBTRACT)
        nc.scalar.activation(f2_early[:].indirect(entries(list5, 0, HALF)), r_low[:], COPY)
        nc.vector.tensor_tensor(r_high[:], bb[:].indirect(entries(list4, HALF, SLOTS)), v[:, HALF:SLOTS], SUBTRACT)
        nc.scalar.activation(f2_late[:].indirect(entries(list5, HALF, SLOTS)), r_high[:], COPY)

        a_early = keep.tile([P, TOKENS], F32)
        nc.vector.tensor_tensor(a_early[:], a[:], f2_early[:], SUBTRACT)
        aa = keep.tile([P, TOKENS], F32)
        nc.vector.tensor_tensor(aa[:], a_early[:], f2_late[:], SUBTRACT)

        y_low = keep.tile([P, HALF], F32)
        aa_high = keep.tile([P, HALF], F32)
        y_high = keep.tile([P, HALF], F32)
        nc.vector.tensor_tensor(y_low[:], aa[:].indirect(entries(list6, 0, HALF)), w[:, 0:HALF], ADD)
        nc.scalar.activation(aa_high[:], aa[:].indirect(entries(list6, HALF, SLOTS)), COPY)
        nc.sync.dma_start(out=out[:, 0:HALF], in_=y_low[:])
        nc.vector.tensor_tensor(y_high[:], aa_high[:], w[:, HALF:SLOTS], ADD)
        nc.sync.dma_start(out=out[:, HALF:SLOTS], in_=y_high[:])
